import numpy as np
import ml_dtypes


def mxq(x, axis, fmt="e4m3"):
    dtype, down = {"e4m3": (ml_dtypes.float8_e4m3fn, 7), "e5m2": (ml_dtypes.float8_e5m2, 14)}[fmt]
    v = np.moveaxis(np.asarray(x, np.float32).astype(ml_dtypes.bfloat16).astype(np.float64), axis, -1)
    blocks = v.reshape(v.shape[:-1] + (-1, 32))
    amax = np.abs(blocks).max(-1, keepdims=True)
    byte = np.maximum(np.where(amax > 0, np.frexp(amax)[1] - 1 + 127, 0) - down, 1)
    scale = np.exp2(byte - 127.0)
    codes = (blocks / scale).astype(np.float32).astype(dtype).astype(np.float64)
    return np.moveaxis((codes * scale).reshape(v.shape), -1, axis)


WIDE = False


def mx_kscale(k):
    if not WIDE:
        return np.ones(k)
    levels = np.array([10, -10, 5, -5, 0])
    if k % 512:
        return np.exp2(np.random.permutation(np.resize(levels, k // 32))).repeat(32)
    a = np.empty((k // 512, 16))
    for p in range(k // 512):
        a[p, :8] = np.random.permutation(np.resize(levels, 8))
        for g in range(8):
            far = levels[np.abs(levels - a[p, g]) >= 10]
            a[p, g + 8] = far[np.random.randint(len(far))]
    return np.exp2(a.ravel()).repeat(32)


def f64(x):
    return np.asarray(x).astype(np.float64)


def striped(idx):
    return np.tile(idx.reshape(-1, 16).T, (8, 1)).astype(np.uint16)


def unstriped(offs):
    return offs[:16].T.reshape(-1).astype(np.int64)


def striped8(idx):
    return np.concatenate([x.reshape(-1, 16).T for x in idx]).astype(np.uint16)


def runs(offs, k):
    lists = np.stack([offs[16 * r : 16 * r + 16].T.reshape(-1) for r in range(8)]).astype(np.int64)
    return lists[np.arange(k) % 512 // 64]


def pack_weight(w):
    k, n = w.shape
    w = f64(np.asarray(w, np.float32).astype(ml_dtypes.bfloat16)).reshape(k // 32, 32, n)
    amax = np.abs(w).max(1)
    byte = np.clip(np.where(amax > 0, np.frexp(amax)[1] - 1 + 127 - 7, 1), 1, 254)
    scaled = (w * np.exp2(127.0 - byte)[:, None, :]).reshape(k, n).astype(np.float32)
    words = np.ascontiguousarray(scaled.reshape(k // 512, 128, 4, n).transpose(0, 1, 3, 2)).astype(ml_dtypes.float8_e4m3fn).view(np.uint8)
    return words, np.ascontiguousarray(byte.astype(np.uint8).reshape(k // 512, 16, n))


def unpack_weight(words, scales):
    g, p, n, _ = words.shape
    vals = np.ascontiguousarray(words).view(ml_dtypes.float8_e4m3fn).astype(np.float64) * np.repeat(np.exp2(scales.astype(np.float64) - 127.0), 8, axis=1)[..., None]
    return vals.transpose(0, 1, 3, 2).reshape(g * 512, n)


def sigmoid(v):
    return 1.0 / (1.0 + np.exp(-np.maximum(v, -700.0)))


K, T, S, G, H, W, C, U = 512, 1024, 256, 2048, 512, 128, 512, 1024


def setup_inputs():
    n = np.random.standard_normal
    s = mx_kscale(K)[:, None]
    packed_xT = pack_weight(n((K, T)) * s)
    packed_dT = pack_weight(n((K, G)) / s)
    perm = np.random.permutation(S)
    return {
        "x_words": packed_xT[0],
        "x_scales": packed_xT[1],
        "d_words": packed_dT[0],
        "d_scales": packed_dT[1],
        "gs": (np.random.uniform(0.5, 1.5, (K, 1)) / s).astype(np.float32),
        "offs": striped(np.random.permutation(T)[:S]),
        "k1": striped8(np.random.randint(0, G, (8, H))),
        "n1": striped(perm[:W]),
        "n2": striped(perm[W:]),
        "cand": striped(np.random.permutation(T)[:C]),
        "n3": striped(np.random.randint(0, S, U)),
    }


def reference(x_words, x_scales, d_words, d_scales, gs, offs, k1, n1, n2, cand, n3):
    x_cand = unpack_weight(x_words, x_scales)[:, unstriped(cand)]
    d_k1 = unpack_weight(d_words, d_scales)[np.arange(K)[:, None], runs(k1, K)]
    xq = unpack_weight(x_words, x_scales)[:, unstriped(offs)]
    h = 0.0625 * (d_k1.T @ xq)
    pb = h[:, unstriped(n2)]
    pa = h[:, unstriped(n1)]
    rb = pb * sigmoid(pb - pa)
    ra = pa * sigmoid(pa - pb)
    ds = np.zeros((H, S))
    ds[:, unstriped(n1)] = ra
    dt = ds.copy()
    dt[:, unstriped(n2)] = rb
    z = f64(gs) * dt
    s = 0.0625 * ((x_cand.T @ mxq(z, 0, "e4m3")))
    mb = s[:, unstriped(n3)]
    mn = mb.reshape(C, S, 4).min(axis=2)
    mx = mb.reshape(C, S, 4).max(axis=2)
    return np.maximum(s, mn) - (0.5 * mx)

@@ -1,0 +1,207 @@
+from contextlib import ExitStack
+
+import concourse.mybir as mybir
+
+K, T, S, G, H, W, C, U = 512, 1024, 256, 2048, 512, 128, 512, 1024
+FLOPS = 2 * K * H * S + 2 * H * C * S
+
+F32 = mybir.dt.float32
+BF16 = mybir.dt.bfloat16
+I32 = mybir.dt.int32
+U32 = mybir.dt.uint32
+U16 = mybir.dt.uint16
+U8 = mybir.dt.uint8
+FP8X4 = mybir.dt.float8_e4m3fn_x4
+ALU = mybir.AluOpType
+ACT = mybir.ActivationFunctionType
+
+P = 128
+PACK = 4
+MEMBERS = 4
+PIECE = 512
+S_WINDOW = PIECE + 16
+
+
+def tile_picked_pqcduelgmid_none_p_kernel(
+    tc, x_words, x_scales, d_words, d_scales, gs, offs, k1, n1, n2, cand, n3, out
+):
+    nc = tc.nc
+    with ExitStack() as ctx:
+        lists = ctx.enter_context(tc.tile_pool(name="lists", bufs=1))
+        sb = ctx.enter_context(tc.tile_pool(name="sb", bufs=1))
+        psum = ctx.enter_context(tc.psum_pool(name="psum", bufs=1))
+
+        def load_list(name, src):
+            tile = lists.tile(list(src.shape), U16, name=name)
+            nc.sync.dma_start(tile[:], src)
+            return tile
+
+        d_bytes = sb.tile([P, G], U8, name="d_bytes")
+        x_bytes = sb.tile([P, T], U8, name="x_bytes")
+        d_table = sb.tile([P, G], U32, name="d_table")
+        x_table = sb.tile([P, T], U32, name="x_table")
+
+        k1_sb = load_list("k1_sb", k1)
+        d_rows = d_scales[0].bitcast(I32)
+        nc.sync.dma_start(
+            d_bytes[:].bitcast(I32),
+            d_rows.unsqueeze(1).broadcast_to([16, 8, G // 4]),
+        )
+        offs_sb = load_list("offs_sb", offs)
+        x_rows = x_scales[0].bitcast(I32)
+        nc.sync.dma_start(
+            x_bytes[:].bitcast(I32),
+            x_rows.unsqueeze(1).broadcast_to([16, 8, T // 4]),
+        )
+        n1_sb = load_list("n1_sb", n1)
+        nc.sync.dma_start(d_table[:].bitcast(I32), d_words[0].rearrange("p n t -> p (n t)").bitcast(I32))
+        nc.sync.dma_start(x_table[:].bitcast(I32), x_words[0].rearrange("p n t -> p (n t)").bitcast(I32))
+        n2_sb = load_list("n2_sb", n2)
+        cand_sb = load_list("cand_sb", cand)
+        n3_sb = load_list("n3_sb", n3)
+        gain = sb.tile([P, PACK], F32, name="gain")
+        nc.gpsimd.dma_start(gain[:], gs.rearrange("(p t) o -> p (t o)", t=PACK))
+
+        s_rows = [sb.tile([P, S_WINDOW], F32, name=f"s_rows{c}") for c in range(C // P)]
+        for c in range(C // P):
+            nc.vector.memset(s_rows[c][:, S:], 0.0)
+
+        def to_plane(spread, width, name, queues):
+            plane = sb.tile([P, width], U8, name=name, align_bytes=64)
+            nc.vector.tensor_copy(plane[:].bitcast(I32), spread[:].bitcast(I32))
+            for e, queue in zip((1, 2, 3), queues):
+                queue.dma_start(plane[:].bitcast(I32)[e:P:32, :], spread[:].bitcast(I32)[8 * e : P : 32, :])
+            return plane
+
+        dk_bytes = sb.tile([P, H], U8, name="dk_bytes")
+        nc.vector.tensor_copy(dk_bytes[:], d_bytes[:].indirect(k1_sb[:]))
+        xq_bytes = sb.tile([P, S], U8, name="xq_bytes")
+        nc.vector.tensor_copy(xq_bytes[:], x_bytes[:].indirect(offs_sb[:]))
+        first_bytes = sb.tile([P, H + S], U8, name="first_bytes")
+        nc.vector.tensor_copy(
+            first_bytes[:, :H].rearrange("p (t m) -> p t m", t=PACK),
+            dk_bytes[:].rearrange("p (m t) -> p t m", t=PACK),
+        )
+        nc.vector.tensor_copy(first_bytes[:, H:].bitcast(I32), xq_bytes[:].bitcast(I32))
+        first_plane = to_plane(first_bytes, H + S, "first_plane", (nc.scalar, nc.sync, nc.scalar))
+
+        dk_words = sb.tile([P, H], U32, name="dk_words")
+        nc.vector.tensor_copy(dk_words[:], d_table[:].indirect(k1_sb[:]))
+        dk_dealt = sb.tile([P, H], U32, name="dk_dealt", align_bytes=64)
+        nc.vector.tensor_copy(
+            dk_dealt[:].bitcast(I32).rearrange("p (t m) -> p t m", t=PACK),
+            dk_words[:].bitcast(I32).rearrange("p (m t) -> p t m", t=PACK),
+        )
+        xq_words = sb.tile([P, S], U32, name="xq_words", align_bytes=64)
+        nc.vector.tensor_copy(xq_words[:], x_table[:].indirect(offs_sb[:]))
+
+        h_rows, pairs, sig, duel, dt_rows = [], [], [], [], []
+        for t in range(PACK):
+            cols = slice(t * P, (t + 1) * P)
+            acc = psum.tile([P, S], F32, name=f"h_acc{t}")
+            nc.tensor.matmul_mx(
+                out=acc[:], lhsT=dk_dealt[:, cols].bitcast(FP8X4), lhsT_scale=first_plane[:, cols],
+                rhs=xq_words[:].bitcast(FP8X4), rhs_scale=first_plane[:, H:], start=True, stop=True,
+            )
+            h_rows.append(sb.tile([P, S], F32, name=f"h_rows{t}"))
+            nc.vector.tensor_scalar(h_rows[t][:], acc[:], 0.0625, None, ALU.mult)
+
+        z_grouped = sb.tile([P, S, PACK], BF16, name="z_grouped", align_bytes=64)
+
+        def fetch_pairs(t):
+            pairs.append(sb.tile([P, 2, W], F32, name=f"pairs{t}", tag=f"pairs{t}", align_bytes=64))
+            nc.scalar.activation(pairs[t][:, 0, :], h_rows[t][:].indirect(n1_sb[:]), ACT.Copy)
+            nc.scalar.activation(pairs[t][:, 1, :], h_rows[t][:].indirect(n2_sb[:]), ACT.Copy)
+            lead = sb.tile([P, 2, W], F32, name=f"lead{t}")
+            nc.vector.tensor_tensor(lead[:], pairs[t][:], pairs[t][:, ::-1, :], ALU.subtract)
+            sig.append(lead)
+
+        def weigh(t):
+            share = sb.tile([P, 2, W], F32, name=f"share{t}")
+            nc.scalar.activation(share[:], sig[t][:], ACT.Sigmoid)
+            duel.append(sb.tile([P, 2, W], F32, name=f"duel{t}"))
+            nc.vector.tensor_tensor(duel[t][:], pairs[t][:], share[:], ALU.mult)
+
+        def put_back(t):
+            dt_rows.append(sb.tile([P, S], F32, name=f"dt_rows{t}"))
+            nc.scalar.activation(dt_rows[t][:].indirect(n1_sb[:]), duel[t][:, 0, :], ACT.Copy)
+            nc.scalar.activation(dt_rows[t][:].indirect(n2_sb[:]), duel[t][:, 1, :], ACT.Copy)
+
+        def group(t, cols):
+            nc.vector.tensor_scalar(z_grouped[:, cols, t], dt_rows[t][:, cols], gain[:, t : t + 1], None, ALU.mult)
+
+
+        for step in range(PACK + 2):
+            if step < PACK:
+                fetch_pairs(step)
+            if 1 <= step <= PACK:
+                weigh(step - 1)
+            if step >= 2:
+                put_back(step - 2)
+                if step - 2 < PACK - 1:
+                    group(step - 2, slice(0, S))
+            if step == 2:
+                xc_bytes = sb.tile([P, C], U8, name="xc_bytes", tag="pairs0", align_bytes=64)
+                nc.vector.tensor_copy(xc_bytes[:], x_bytes[:].indirect(cand_sb[:]))
+                xc_plane = to_plane(xc_bytes, C, "xc_plane", (nc.sync, nc.sync, nc.sync))
+            if step == 3:
+                xc_words = sb.tile([P, C], U32, name="xc_words", tag="pairs1", align_bytes=64)
+                nc.vector.tensor_copy(xc_words[:], x_table[:].indirect(cand_sb[:]))
+
+        z_words = sb.tile([P, S], U32, name="z_words", align_bytes=64)
+        z_plane = sb.tile([P, S], U8, name="z_plane", align_bytes=64)
+        halves = [slice(0, S // 2), slice(S // 2, S)]
+        for cols in halves:
+            group(PACK - 1, cols)
+        for cols in halves:
+            nc.vector.quantize_mx(
+                out=z_words[:, cols].bitcast(FP8X4), scales=z_plane[:, cols],
+                in_=z_grouped[:, cols, :].rearrange("p w t -> p (w t)"),
+            )
+
+        for c in range(C // P):
+            cols = slice(c * P, (c + 1) * P)
+            acc = psum.tile([P, S], F32, name=f"s_acc{c}")
+            nc.tensor.matmul_mx(
+                out=acc[:], lhsT=xc_words[:, cols].bitcast(FP8X4), lhsT_scale=xc_plane[:, cols],
+                rhs=z_words[:].bitcast(FP8X4), rhs_scale=z_plane[:], start=True, stop=True,
+            )
+            if c == 0:
+                nc.scalar.activation(s_rows[c][:, :S], acc[:], ACT.Copy, scale=0.0625)
+            else:
+                nc.vector.tensor_scalar(s_rows[c][:, :S], acc[:], 0.0625, None, ALU.mult)
+
+        width = PIECE // MEMBERS
+        mb = [sb.tile([P, S, MEMBERS], F32, name=f"mb{c}") for c in range(C // P)]
+        for c in range(C // P):
+            for u in range(U // PIECE):
+                nc.scalar.activation(
+                    mb[c][:, u * width : (u + 1) * width, :].rearrange("p j t -> p (j t)"),
+                    s_rows[c][:].indirect(n3_sb[:, u * PIECE // 16 : (u + 1) * PIECE // 16]),
+                    ACT.Copy,
+                )
+
+        stretches = [(0, slice(0, width)), (0, slice(width, S))] + [(c, slice(0, S)) for c in range(1, C // P)]
+        finish = None
+        for c, cols in stretches:
+            n = cols.stop - cols.start
+            name = f"{c}_{cols.start}"
+            low2 = sb.tile([P, n, 2], F32, name="low2" + name)
+            high2 = sb.tile([P, n, 2], F32, name="high2" + name)
+            low = sb.tile([P, n], F32, name="low" + name)
+            high = sb.tile([P, n], F32, name="high" + name)
+            kept = sb.tile([P, n], F32, name="kept" + name)
+            nc.vector.tensor_tensor(low2[:], mb[c][:, cols, 0:2], mb[c][:, cols, 2:4], ALU.min)
+            if finish is not None:
+                finish()
+            nc.vector.tensor_tensor(high2[:], mb[c][:, cols, 0:2], mb[c][:, cols, 2:4], ALU.max)
+            nc.vector.tensor_tensor(low[:], low2[:, :, 0], low2[:, :, 1], ALU.min)
+            nc.vector.tensor_tensor(high[:], high2[:, :, 0], high2[:, :, 1], ALU.max)
+            nc.vector.tensor_tensor(kept[:], low[:], s_rows[c][:, cols], ALU.max)
+
+            def finish(c=c, cols=cols, n=n, name=name, high=high, kept=kept):
+                result = sb.tile([P, n], F32, name="result" + name)
+                nc.vector.scalar_tensor_tensor(result[:], high[:], -0.5, kept[:], ALU.mult, ALU.add)
+                nc.sync.dma_start(out[c * P : (c + 1) * P, cols], result[:])
+
+        finish()

@@ -41,22 +41,18 @@ def tile_picked_pqcduelgmid_none_p_kernel(
         d_table = sb.tile([P, G], U32, name="d_table")
         x_table = sb.tile([P, T], U32, name="x_table")
 
-        k1_sb = load_list("k1_sb", k1)
-        d_rows = d_scales[0].bitcast(I32)
-        nc.sync.dma_start(
-            d_bytes[:].bitcast(I32),
-            d_rows.unsqueeze(1).broadcast_to([16, 8, G // 4]),
-        )
+        def load_scale_rows(tile, scales, width):
+            rows = scales[0].bitcast(I32)
+            nc.sync.dma_start(tile[:].bitcast(I32), rows.unsqueeze(1).broadcast_to([16, 8, width // 4]))
+
         offs_sb = load_list("offs_sb", offs)
-        x_rows = x_scales[0].bitcast(I32)
-        nc.sync.dma_start(
-            x_bytes[:].bitcast(I32),
-            x_rows.unsqueeze(1).broadcast_to([16, 8, T // 4]),
-        )
+        load_scale_rows(x_bytes, x_scales, T)
+        k1_sb = load_list("k1_sb", k1)
+        load_scale_rows(d_bytes, d_scales, G)
         n1_sb = load_list("n1_sb", n1)
+        n2_sb = load_list("n2_sb", n2)
         nc.sync.dma_start(d_table[:].bitcast(I32), d_words[0].rearrange("p n t -> p (n t)").bitcast(I32))
         nc.sync.dma_start(x_table[:].bitcast(I32), x_words[0].rearrange("p n t -> p (n t)").bitcast(I32))
-        n2_sb = load_list("n2_sb", n2)
         cand_sb = load_list("cand_sb", cand)
         n3_sb = load_list("n3_sb", n3)
         gain = sb.tile([P, PACK], F32, name="gain")
@@ -66,24 +62,16 @@ def tile_picked_pqcduelgmid_none_p_kernel(
         for c in range(C // P):
             nc.vector.memset(s_rows[c][:, S:], 0.0)
 
-        def to_plane(spread, width, name, queues):
-            plane = sb.tile([P, width], U8, name=name, align_bytes=64)
-            nc.vector.tensor_copy(plane[:].bitcast(I32), spread[:].bitcast(I32))
-            for e, queue in zip((1, 2, 3), queues):
+        def to_plane(plane, spread, queues):
+            for e, queue in enumerate(queues):
                 queue.dma_start(plane[:].bitcast(I32)[e:P:32, :], spread[:].bitcast(I32)[8 * e : P : 32, :])
-            return plane
 
-        dk_bytes = sb.tile([P, H], U8, name="dk_bytes")
-        nc.vector.tensor_copy(dk_bytes[:], d_bytes[:].indirect(k1_sb[:]))
-        xq_bytes = sb.tile([P, S], U8, name="xq_bytes")
-        nc.vector.tensor_copy(xq_bytes[:], x_bytes[:].indirect(offs_sb[:]))
-        first_bytes = sb.tile([P, H + S], U8, name="first_bytes")
-        nc.vector.tensor_copy(
-            first_bytes[:, :H].rearrange("p (t m) -> p t m", t=PACK),
-            dk_bytes[:].rearrange("p (m t) -> p t m", t=PACK),
-        )
-        nc.vector.tensor_copy(first_bytes[:, H:].bitcast(I32), xq_bytes[:].bitcast(I32))
-        first_plane = to_plane(first_bytes, H + S, "first_plane", (nc.scalar, nc.sync, nc.scalar))
+        first_plane = sb.tile([P, S + H], U8, name="first_plane", align_bytes=64)
+        nc.vector.memset(first_plane[:].bitcast(I32), 0)
+        first_bytes = sb.tile([P, S + H], U8, name="first_bytes")
+        nc.vector.tensor_copy(first_bytes[:, :S], x_bytes[:].indirect(offs_sb[:]))
+        nc.vector.tensor_copy(first_bytes[:, S:], d_bytes[:].indirect(k1_sb[:]))
+        to_plane(first_plane, first_bytes, (nc.scalar, nc.sync, nc.scalar, nc.sync))
 
         dk_words = sb.tile([P, H], U32, name="dk_words")
         nc.vector.tensor_copy(dk_words[:], d_table[:].indirect(k1_sb[:]))
@@ -94,14 +82,19 @@ def tile_picked_pqcduelgmid_none_p_kernel(
         )
         xq_words = sb.tile([P, S], U32, name="xq_words", align_bytes=64)
         nc.vector.tensor_copy(xq_words[:], x_table[:].indirect(offs_sb[:]))
+        dk_plane = sb.tile([P, H], U8, name="dk_plane", align_bytes=64)
+        nc.vector.tensor_copy(
+            dk_plane[:].rearrange("p (t m) -> p t m", t=PACK),
+            first_plane[:, S:].rearrange("p (m t) -> p t m", t=PACK),
+        )
 
         h_rows, pairs, sig, duel, dt_rows = [], [], [], [], []
         for t in range(PACK):
             cols = slice(t * P, (t + 1) * P)
-            acc = psum.tile([P, S], F32, name=f"h_acc{t}")
+            acc = psum.tile([P, S], F32, name=f"h_acc{t}", tag=f"h_acc{t}")
             nc.tensor.matmul_mx(
-                out=acc[:], lhsT=dk_dealt[:, cols].bitcast(FP8X4), lhsT_scale=first_plane[:, cols],
-                rhs=xq_words[:].bitcast(FP8X4), rhs_scale=first_plane[:, H:], start=True, stop=True,
+                out=acc[:], lhsT=dk_dealt[:, cols].bitcast(FP8X4), lhsT_scale=dk_plane[:, cols],
+                rhs=xq_words[:].bitcast(FP8X4), rhs_scale=first_plane[:, :S], start=True, stop=True,
             )
             h_rows.append(sb.tile([P, S], F32, name=f"h_rows{t}"))
             nc.vector.tensor_scalar(h_rows[t][:], acc[:], 0.0625, None, ALU.mult)
@@ -110,17 +103,18 @@ def tile_picked_pqcduelgmid_none_p_kernel(
 
         def fetch_pairs(t):
             pairs.append(sb.tile([P, 2, W], F32, name=f"pairs{t}", tag=f"pairs{t}", align_bytes=64))
-            nc.scalar.activation(pairs[t][:, 0, :], h_rows[t][:].indirect(n1_sb[:]), ACT.Copy)
-            nc.scalar.activation(pairs[t][:, 1, :], h_rows[t][:].indirect(n2_sb[:]), ACT.Copy)
-            lead = sb.tile([P, 2, W], F32, name=f"lead{t}")
-            nc.vector.tensor_tensor(lead[:], pairs[t][:], pairs[t][:, ::-1, :], ALU.subtract)
+            nc.scalar.activation(pairs[t][:, 0, :], h_rows[t][:].indirect(n1_sb[:]), ACT.Copy, scale=0.5)
+            nc.scalar.activation(pairs[t][:, 1, :], h_rows[t][:].indirect(n2_sb[:]), ACT.Copy, scale=-0.5)
+            lead = sb.tile([P, W], F32, name=f"lead{t}")
+            nc.vector.tensor_tensor(lead[:], pairs[t][:, 0, :], pairs[t][:, 1, :], ALU.add)
             sig.append(lead)
 
         def weigh(t):
-            share = sb.tile([P, 2, W], F32, name=f"share{t}")
-            nc.scalar.activation(share[:], sig[t][:], ACT.Sigmoid)
+            share = sb.tile([P, W], F32, name=f"share{t}")
+            nc.scalar.activation(share[:], sig[t][:], ACT.Tanh)
             duel.append(sb.tile([P, 2, W], F32, name=f"duel{t}"))
-            nc.vector.tensor_tensor(duel[t][:], pairs[t][:], share[:], ALU.mult)
+            nc.vector.scalar_tensor_tensor(duel[t][:, 0, :], share[:], 1.0, pairs[t][:, 0, :], ALU.add, ALU.mult)
+            nc.vector.scalar_tensor_tensor(duel[t][:, 1, :], share[:], 1.0, pairs[t][:, 1, :], ALU.subtract, ALU.mult)
 
         def put_back(t):
             dt_rows.append(sb.tile([P, S], F32, name=f"dt_rows{t}"))
@@ -140,12 +134,13 @@ def tile_picked_pqcduelgmid_none_p_kernel(
                 put_back(step - 2)
                 if step - 2 < PACK - 1:
                     group(step - 2, slice(0, S))
-            if step == 2:
-                xc_bytes = sb.tile([P, C], U8, name="xc_bytes", tag="pairs0", align_bytes=64)
-                nc.vector.tensor_copy(xc_bytes[:], x_bytes[:].indirect(cand_sb[:]))
-                xc_plane = to_plane(xc_bytes, C, "xc_plane", (nc.sync, nc.sync, nc.sync))
             if step == 3:
-                xc_words = sb.tile([P, C], U32, name="xc_words", tag="pairs1", align_bytes=64)
+                xc_bytes = sb.tile([P, C], U8, name="xc_bytes", tag="pairs2", align_bytes=64)
+                nc.vector.tensor_copy(xc_bytes[:], x_bytes[:].indirect(cand_sb[:]))
+                xc_plane = sb.tile([P, C], U8, name="xc_plane", align_bytes=64)
+                to_plane(xc_plane, xc_bytes, (nc.sync,) * 4)
+            if step == 4:
+                xc_words = sb.tile([P, C], U32, name="xc_words", tag="pairs3", align_bytes=64)
                 nc.vector.tensor_copy(xc_words[:], x_table[:].indirect(cand_sb[:]))
 
         z_words = sb.tile([P, S], U32, name="z_words", align_bytes=64)
@@ -159,49 +154,42 @@ def tile_picked_pqcduelgmid_none_p_kernel(
                 in_=z_grouped[:, cols, :].rearrange("p w t -> p (w t)"),
             )
 
-        for c in range(C // P):
-            cols = slice(c * P, (c + 1) * P)
-            acc = psum.tile([P, S], F32, name=f"s_acc{c}")
+        def score(c, cols, tag):
+            rows = slice(c * P, (c + 1) * P)
+            acc = psum.tile([P, cols.stop - cols.start], F32, name=f"s_acc{c}_{cols.start}", tag=tag)
             nc.tensor.matmul_mx(
-                out=acc[:], lhsT=xc_words[:, cols].bitcast(FP8X4), lhsT_scale=xc_plane[:, cols],
-                rhs=z_words[:].bitcast(FP8X4), rhs_scale=z_plane[:], start=True, stop=True,
+                out=acc[:], lhsT=xc_words[:, rows].bitcast(FP8X4), lhsT_scale=xc_plane[:, rows],
+                rhs=z_words[:, cols].bitcast(FP8X4), rhs_scale=z_plane[:, cols], start=True, stop=True,
             )
-            if c == 0:
-                nc.scalar.activation(s_rows[c][:, :S], acc[:], ACT.Copy, scale=0.0625)
-            else:
-                nc.vector.tensor_scalar(s_rows[c][:, :S], acc[:], 0.0625, None, ALU.mult)
+            return acc
 
-        width = PIECE // MEMBERS
-        mb = [sb.tile([P, S, MEMBERS], F32, name=f"mb{c}") for c in range(C // P)]
+        nc.scalar.activation(s_rows[0][:, halves[0]], score(0, halves[0], "s_acc0")[:], ACT.Copy, scale=0.0625)
+        nc.vector.tensor_scalar(s_rows[0][:, halves[1]], score(0, halves[1], "h_acc0")[:], 0.0625, None, ALU.mult)
+        for c in range(1, C // P):
+            nc.vector.tensor_scalar(s_rows[c][:, :S], score(c, slice(0, S), f"s_acc{c}")[:], 0.0625, None, ALU.mult)
+
+        last = C // P - 1
         for c in range(C // P):
-            for u in range(U // PIECE):
+            mb = sb.tile([P, S, MEMBERS], F32, name=f"mb{c}")
+            low2 = sb.tile([P, S, 2], F32, name=f"low2_{c}")
+            high2 = sb.tile([P, S, 2], F32, name=f"high2_{c}")
+            low = sb.tile([P, S], F32, name=f"low{c}")
+            high = sb.tile([P, S], F32, name=f"high{c}")
+            kept = sb.tile([P, S], F32, name=f"kept{c}")
+            result = sb.tile([P, S], F32, name=f"result{c}")
+            cuts = (0, S // 2, S) if c < last else (0, S // 2, 3 * S // 4, S)
+            for j0, j1 in zip(cuts, cuts[1:]):
                 nc.scalar.activation(
-                    mb[c][:, u * width : (u + 1) * width, :].rearrange("p j t -> p (j t)"),
-                    s_rows[c][:].indirect(n3_sb[:, u * PIECE // 16 : (u + 1) * PIECE // 16]),
+                    mb[:, j0:j1, :].rearrange("p j t -> p (j t)"),
+                    s_rows[c][:].indirect(n3_sb[:, j0 * MEMBERS // 16 : j1 * MEMBERS // 16]),
                     ACT.Copy,
                 )
-
-        stretches = [(0, slice(0, width)), (0, slice(width, S))] + [(c, slice(0, S)) for c in range(1, C // P)]
-        finish = None
-        for c, cols in stretches:
-            n = cols.stop - cols.start
-            name = f"{c}_{cols.start}"
-            low2 = sb.tile([P, n, 2], F32, name="low2" + name)
-            high2 = sb.tile([P, n, 2], F32, name="high2" + name)
-            low = sb.tile([P, n], F32, name="low" + name)
-            high = sb.tile([P, n], F32, name="high" + name)
-            kept = sb.tile([P, n], F32, name="kept" + name)
-            nc.vector.tensor_tensor(low2[:], mb[c][:, cols, 0:2], mb[c][:, cols, 2:4], ALU.min)
-            if finish is not None:
-                finish()
-            nc.vector.tensor_tensor(high2[:], mb[c][:, cols, 0:2], mb[c][:, cols, 2:4], ALU.max)
-            nc.vector.tensor_tensor(low[:], low2[:, :, 0], low2[:, :, 1], ALU.min)
-            nc.vector.tensor_tensor(high[:], high2[:, :, 0], high2[:, :, 1], ALU.max)
-            nc.vector.tensor_tensor(kept[:], low[:], s_rows[c][:, cols], ALU.max)
-
-            def finish(c=c, cols=cols, n=n, name=name, high=high, kept=kept):
-                result = sb.tile([P, n], F32, name="result" + name)
-                nc.vector.scalar_tensor_tensor(result[:], high[:], -0.5, kept[:], ALU.mult, ALU.add)
-                nc.sync.dma_start(out[c * P : (c + 1) * P, cols], result[:])
-
-        finish()
+                nc.vector.tensor_tensor(low2[:, j0:j1, :], mb[:, j0:j1, 0:2], mb[:, j0:j1, 2:4], ALU.min)
+                nc.vector.tensor_tensor(high2[:, j0:j1, :], mb[:, j0:j1, 0:2], mb[:, j0:j1, 2:4], ALU.max)
+                if c == last or j1 == S:
+                    cols = slice(j0 if c == last else 0, j1)
+                    nc.vector.tensor_tensor(low[:, cols], low2[:, cols, 0], low2[:, cols, 1], ALU.min)
+                    nc.vector.tensor_tensor(high[:, cols], high2[:, cols, 0], high2[:, cols, 1], ALU.max)
+                    nc.vector.tensor_tensor(kept[:, cols], low[:, cols], s_rows[c][:, cols], ALU.max)
+                    nc.vector.scalar_tensor_tensor(result[:, cols], high[:, cols], -0.5, kept[:, cols], ALU.mult, ALU.add)
+                    nc.sync.dma_start(out[c * P : (c + 1) * P, cols], result[:, cols])

@@ -41,16 +41,15 @@ def tile_picked_pqcduelgmid_none_p_kernel(
         d_table = sb.tile([P, G], U32, name="d_table")
         x_table = sb.tile([P, T], U32, name="x_table")
 
-        def load_scale_rows(tile, scales, width):
-            rows = scales[0].bitcast(I32)
-            nc.sync.dma_start(tile[:].bitcast(I32), rows.unsqueeze(1).broadcast_to([16, 8, width // 4]))
-
+        nc.vector.memset(d_bytes[:].bitcast(I32), 0)
         offs_sb = load_list("offs_sb", offs)
-        load_scale_rows(x_bytes, x_scales, T)
+        nc.sync.dma_start(
+            x_bytes[:].bitcast(I32), x_scales[0].bitcast(I32).unsqueeze(1).broadcast_to([16, 8, T // 4])
+        )
         k1_sb = load_list("k1_sb", k1)
-        load_scale_rows(d_bytes, d_scales, G)
         n1_sb = load_list("n1_sb", n1)
         n2_sb = load_list("n2_sb", n2)
+        nc.sync.dma_start(d_bytes[:].bitcast(I32)[0:P:8, :], d_scales[0].bitcast(I32))
         nc.sync.dma_start(d_table[:].bitcast(I32), d_words[0].rearrange("p n t -> p (n t)").bitcast(I32))
         nc.sync.dma_start(x_table[:].bitcast(I32), x_words[0].rearrange("p n t -> p (n t)").bitcast(I32))
         cand_sb = load_list("cand_sb", cand)
@@ -68,36 +67,47 @@ def tile_picked_pqcduelgmid_none_p_kernel(
 
         first_plane = sb.tile([P, S + H], U8, name="first_plane", align_bytes=64)
         nc.vector.memset(first_plane[:].bitcast(I32), 0)
-        first_bytes = sb.tile([P, S + H], U8, name="first_bytes")
+        first_bytes = sb.tile([P, S + H], U8, name="first_bytes", tag="first_bytes", align_bytes=64)
         nc.vector.tensor_copy(first_bytes[:, :S], x_bytes[:].indirect(offs_sb[:]))
         nc.vector.tensor_copy(first_bytes[:, S:], d_bytes[:].indirect(k1_sb[:]))
         to_plane(first_plane, first_bytes, (nc.scalar, nc.sync, nc.scalar, nc.sync))
 
         dk_words = sb.tile([P, H], U32, name="dk_words")
         nc.vector.tensor_copy(dk_words[:], d_table[:].indirect(k1_sb[:]))
-        dk_dealt = sb.tile([P, H], U32, name="dk_dealt", align_bytes=64)
-        nc.vector.tensor_copy(
-            dk_dealt[:].bitcast(I32).rearrange("p (t m) -> p t m", t=PACK),
-            dk_words[:].bitcast(I32).rearrange("p (m t) -> p t m", t=PACK),
-        )
         xq_words = sb.tile([P, S], U32, name="xq_words", align_bytes=64)
-        nc.vector.tensor_copy(xq_words[:], x_table[:].indirect(offs_sb[:]))
-        dk_plane = sb.tile([P, H], U8, name="dk_plane", align_bytes=64)
-        nc.vector.tensor_copy(
-            dk_plane[:].rearrange("p (t m) -> p t m", t=PACK),
-            first_plane[:, S:].rearrange("p (m t) -> p t m", t=PACK),
-        )
+        halves = [slice(0, S // 2), slice(S // 2, S)]
 
-        h_rows, pairs, sig, duel, dt_rows = [], [], [], [], []
-        for t in range(PACK):
-            cols = slice(t * P, (t + 1) * P)
-            acc = psum.tile([P, S], F32, name=f"h_acc{t}", tag=f"h_acc{t}")
-            nc.tensor.matmul_mx(
-                out=acc[:], lhsT=dk_dealt[:, cols].bitcast(FP8X4), lhsT_scale=dk_plane[:, cols],
-                rhs=xq_words[:].bitcast(FP8X4), rhs_scale=first_plane[:, :S], start=True, stop=True,
+        def deal_words(t0, tag):
+            dealt = sb.tile([P, 2, P], U32, name=f"dk_dealt{t0}", tag=tag, align_bytes=64)
+            nc.vector.tensor_copy(
+                dealt[:].bitcast(I32).rearrange("p t m -> p m t"),
+                dk_words[:].bitcast(I32).rearrange("p (m t) -> p m t", t=PACK)[:, :, t0 : t0 + 2],
             )
-            h_rows.append(sb.tile([P, S], F32, name=f"h_rows{t}"))
-            nc.vector.tensor_scalar(h_rows[t][:], acc[:], 0.0625, None, ALU.mult)
+            return [dealt[:, 0, :], dealt[:, 1, :]]
+
+        def deal_bytes(t):
+            dealt = sb.tile([P, P], U8, name=f"dk_plane{t}", align_bytes=64)
+            nc.vector.tensor_copy(dealt[:], first_plane[:, S + t :: PACK])
+            return dealt[:]
+
+        dk_dealt = deal_words(0, "dk_dealt0")
+        nc.vector.tensor_copy(xq_words[:], x_table[:].indirect(offs_sb[:]))
+        dk_plane = [deal_bytes(0), deal_bytes(1)]
+        dk_dealt.extend(deal_words(2, "first_bytes"))
+        dk_plane.extend([deal_bytes(2), deal_bytes(3)])
+
+        def layer(t, cols, tag):
+            acc = psum.tile([P, cols.stop - cols.start], F32, name=f"h_acc{t}_{cols.start}", tag=tag)
+            nc.tensor.matmul_mx(
+                out=acc[:], lhsT=dk_dealt[t].bitcast(FP8X4), lhsT_scale=dk_plane[t],
+                rhs=xq_words[:, cols].bitcast(FP8X4), rhs_scale=first_plane[:, cols], start=True, stop=True,
+            )
+            return acc
+
+        pairs, sig, duel, dt_rows = [], [], [], []
+        h_rows = [sb.tile([P, S], F32, name=f"h_rows{t}") for t in range(PACK)]
+        for t in range(PACK):
+            nc.vector.tensor_scalar(h_rows[t][:], layer(t, slice(0, S), f"h_acc{t}")[:], 0.0625, None, ALU.mult)
 
         z_grouped = sb.tile([P, S, PACK], BF16, name="z_grouped", align_bytes=64)
 
@@ -145,7 +155,6 @@ def tile_picked_pqcduelgmid_none_p_kernel(
 
         z_words = sb.tile([P, S], U32, name="z_words", align_bytes=64)
         z_plane = sb.tile([P, S], U8, name="z_plane", align_bytes=64)
-        halves = [slice(0, S // 2), slice(S // 2, S)]
         for cols in halves:
             group(PACK - 1, cols)
         for cols in halves:
@@ -169,6 +178,7 @@ def tile_picked_pqcduelgmid_none_p_kernel(
             nc.vector.tensor_scalar(s_rows[c][:, :S], score(c, slice(0, S), f"s_acc{c}")[:], 0.0625, None, ALU.mult)
 
         last = C // P - 1
+        pending = []
         for c in range(C // P):
             mb = sb.tile([P, S, MEMBERS], F32, name=f"mb{c}")
             low2 = sb.tile([P, S, 2], F32, name=f"low2_{c}")
@@ -177,7 +187,13 @@ def tile_picked_pqcduelgmid_none_p_kernel(
             high = sb.tile([P, S], F32, name=f"high{c}")
             kept = sb.tile([P, S], F32, name=f"kept{c}")
             result = sb.tile([P, S], F32, name=f"result{c}")
-            cuts = (0, S // 2, S) if c < last else (0, S // 2, 3 * S // 4, S)
+
+            def finish(cols, c=c, high=high, kept=kept, result=result):
+                nc.vector.scalar_tensor_tensor(result[:, cols], high[:, cols], -0.5, kept[:, cols], ALU.mult, ALU.add)
+                nc.sync.dma_start(out[c * P : (c + 1) * P, cols], result[:, cols])
+
+            cuts = (0, S // 4, S // 2, S) if c == 0 else (0, S // 2, S)
+            done = 0
             for j0, j1 in zip(cuts, cuts[1:]):
                 nc.scalar.activation(
                     mb[:, j0:j1, :].rearrange("p j t -> p (j t)"),
@@ -185,11 +201,17 @@ def tile_picked_pqcduelgmid_none_p_kernel(
                     ACT.Copy,
                 )
                 nc.vector.tensor_tensor(low2[:, j0:j1, :], mb[:, j0:j1, 0:2], mb[:, j0:j1, 2:4], ALU.min)
+                for call, cols in pending:
+                    call(cols)
+                pending.clear()
                 nc.vector.tensor_tensor(high2[:, j0:j1, :], mb[:, j0:j1, 0:2], mb[:, j0:j1, 2:4], ALU.max)
-                if c == last or j1 == S:
-                    cols = slice(j0 if c == last else 0, j1)
+                if j1 == S or (c == 0 and j1 == S // 2):
+                    cols = slice(done, j1)
+                    done = j1
                     nc.vector.tensor_tensor(low[:, cols], low2[:, cols, 0], low2[:, cols, 1], ALU.min)
                     nc.vector.tensor_tensor(high[:, cols], high2[:, cols, 0], high2[:, cols, 1], ALU.max)
-                    nc.vector.tensor_tensor(kept[:, cols], low[:, cols], s_rows[c][:, cols], ALU.max)
-                    nc.vector.scalar_tensor_tensor(result[:, cols], high[:, cols], -0.5, kept[:, cols], ALU.mult, ALU.add)
-                    nc.sync.dma_start(out[c * P : (c + 1) * P, cols], result[:, cols])
+                    for part in halves if c == last else [cols]:
+                        nc.vector.tensor_tensor(kept[:, part], low[:, part], s_rows[c][:, part], ALU.max)
+                        pending.append((finish, part))
+        for call, cols in pending:
+            call(cols)

@@ -190,7 +190,8 @@ def tile_picked_pqcduelgmid_none_p_kernel(
 
             def finish(cols, c=c, high=high, kept=kept, result=result):
                 nc.vector.scalar_tensor_tensor(result[:, cols], high[:, cols], -0.5, kept[:, cols], ALU.mult, ALU.add)
-                nc.sync.dma_start(out[c * P : (c + 1) * P, cols], result[:, cols])
+                queue = nc.scalar if c == last and cols.stop == S else nc.sync
+                queue.dma_start(out[c * P : (c + 1) * P, cols], result[:, cols])
 
             cuts = (0, S // 4, S // 2, S) if c == 0 else (0, S // 2, S)
             done = 0
@@ -200,11 +201,11 @@ def tile_picked_pqcduelgmid_none_p_kernel(
                     s_rows[c][:].indirect(n3_sb[:, j0 * MEMBERS // 16 : j1 * MEMBERS // 16]),
                     ACT.Copy,
                 )
-                nc.vector.tensor_tensor(low2[:, j0:j1, :], mb[:, j0:j1, 0:2], mb[:, j0:j1, 2:4], ALU.min)
+                nc.vector.tensor_tensor(low2[:, j0:j1, :], mb[:, j0:j1, 0::2], mb[:, j0:j1, 1::2], ALU.min)
                 for call, cols in pending:
                     call(cols)
                 pending.clear()
-                nc.vector.tensor_tensor(high2[:, j0:j1, :], mb[:, j0:j1, 0:2], mb[:, j0:j1, 2:4], ALU.max)
+                nc.vector.tensor_tensor(high2[:, j0:j1, :], mb[:, j0:j1, 0::2], mb[:, j0:j1, 1::2], ALU.max)
                 if j1 == S or (c == 0 and j1 == S // 2):
                     cols = slice(done, j1)
                     done = j1

from contextlib import ExitStack

import concourse.mybir as mybir

K, T, S, G, H, W, C, U = 512, 1024, 256, 2048, 512, 128, 512, 1024
FLOPS = 2 * K * H * S + 2 * H * C * S

F32 = mybir.dt.float32
BF16 = mybir.dt.bfloat16
I32 = mybir.dt.int32
U32 = mybir.dt.uint32
U16 = mybir.dt.uint16
U8 = mybir.dt.uint8
FP8X4 = mybir.dt.float8_e4m3fn_x4
ALU = mybir.AluOpType
ACT = mybir.ActivationFunctionType

P = 128
PACK = 4
MEMBERS = 4
PIECE = 512
S_WINDOW = PIECE + 16


def tile_picked_pqcduelgmid_none_p_kernel(
    tc, x_words, x_scales, d_words, d_scales, gs, offs, k1, n1, n2, cand, n3, out
):
    nc = tc.nc
    with ExitStack() as ctx:
        lists = ctx.enter_context(tc.tile_pool(name="lists", bufs=1))
        sb = ctx.enter_context(tc.tile_pool(name="sb", bufs=1))
        psum = ctx.enter_context(tc.psum_pool(name="psum", bufs=1))

        def load_list(name, src):
            tile = lists.tile(list(src.shape), U16, name=name)
            nc.sync.dma_start(tile[:], src)
            return tile

        d_bytes = sb.tile([P, G], U8, name="d_bytes")
        x_bytes = sb.tile([P, T], U8, name="x_bytes")
        d_table = sb.tile([P, G], U32, name="d_table")
        x_table = sb.tile([P, T], U32, name="x_table")

        nc.vector.memset(d_bytes[:].bitcast(I32), 0)
        offs_sb = load_list("offs_sb", offs)
        nc.sync.dma_start(
            x_bytes[:].bitcast(I32), x_scales[0].bitcast(I32).unsqueeze(1).broadcast_to([16, 8, T // 4])
        )
        k1_sb = load_list("k1_sb", k1)
        n1_sb = load_list("n1_sb", n1)
        n2_sb = load_list("n2_sb", n2)
        nc.sync.dma_start(d_bytes[:].bitcast(I32)[0:P:8, :], d_scales[0].bitcast(I32))
        nc.sync.dma_start(d_table[:].bitcast(I32), d_words[0].rearrange("p n t -> p (n t)").bitcast(I32))
        nc.sync.dma_start(x_table[:].bitcast(I32), x_words[0].rearrange("p n t -> p (n t)").bitcast(I32))
        cand_sb = load_list("cand_sb", cand)
        n3_sb = load_list("n3_sb", n3)
        gain = sb.tile([P, PACK], F32, name="gain")
        nc.gpsimd.dma_start(gain[:], gs.rearrange("(p t) o -> p (t o)", t=PACK))

        s_rows = [sb.tile([P, S_WINDOW], F32, name=f"s_rows{c}") for c in range(C // P)]
        for c in range(C // P):
            nc.vector.memset(s_rows[c][:, S:], 0.0)

        def to_plane(plane, spread, queues):
            for e, queue in enumerate(queues):
                queue.dma_start(plane[:].bitcast(I32)[e:P:32, :], spread[:].bitcast(I32)[8 * e : P : 32, :])

        first_plane = sb.tile([P, S + H], U8, name="first_plane", align_bytes=64)
        nc.vector.memset(first_plane[:].bitcast(I32), 0)
        first_bytes = sb.tile([P, S + H], U8, name="first_bytes", tag="first_bytes", align_bytes=64)
        nc.vector.tensor_copy(first_bytes[:, :S], x_bytes[:].indirect(offs_sb[:]))
        nc.vector.tensor_copy(first_bytes[:, S:], d_bytes[:].indirect(k1_sb[:]))
        to_plane(first_plane, first_bytes, (nc.scalar, nc.sync, nc.scalar, nc.sync))

        dk_words = sb.tile([P, H], U32, name="dk_words")
        nc.vector.tensor_copy(dk_words[:], d_table[:].indirect(k1_sb[:]))
        xq_words = sb.tile([P, S], U32, name="xq_words", align_bytes=64)
        halves = [slice(0, S // 2), slice(S // 2, S)]

        def deal_words(t0, tag):
            dealt = sb.tile([P, 2, P], U32, name=f"dk_dealt{t0}", tag=tag, align_bytes=64)
            nc.vector.tensor_copy(
                dealt[:].bitcast(I32).rearrange("p t m -> p m t"),
                dk_words[:].bitcast(I32).rearrange("p (m t) -> p m t", t=PACK)[:, :, t0 : t0 + 2],
            )
            return [dealt[:, 0, :], dealt[:, 1, :]]

        def deal_bytes(t):
            dealt = sb.tile([P, P], U8, name=f"dk_plane{t}", align_bytes=64)
            nc.vector.tensor_copy(dealt[:], first_plane[:, S + t :: PACK])
            return dealt[:]

        dk_dealt = deal_words(0, "dk_dealt0")
        nc.vector.tensor_copy(xq_words[:], x_table[:].indirect(offs_sb[:]))
        dk_plane = [deal_bytes(0), deal_bytes(1)]
        dk_dealt.extend(deal_words(2, "first_bytes"))
        dk_plane.extend([deal_bytes(2), deal_bytes(3)])

        def layer(t, cols, tag):
            acc = psum.tile([P, cols.stop - cols.start], F32, name=f"h_acc{t}_{cols.start}", tag=tag)
            nc.tensor.matmul_mx(
                out=acc[:], lhsT=dk_dealt[t].bitcast(FP8X4), lhsT_scale=dk_plane[t],
                rhs=xq_words[:, cols].bitcast(FP8X4), rhs_scale=first_plane[:, cols], start=True, stop=True,
            )
            return acc

        pairs, sig, duel, dt_rows = [], [], [], []
        h_rows = [sb.tile([P, S], F32, name=f"h_rows{t}") for t in range(PACK)]
        for t in range(PACK):
            nc.vector.tensor_scalar(h_rows[t][:], layer(t, slice(0, S), f"h_acc{t}")[:], 0.0625, None, ALU.mult)

        z_grouped = sb.tile([P, S, PACK], BF16, name="z_grouped", align_bytes=64)

        def fetch_pairs(t):
            pairs.append(sb.tile([P, 2, W], F32, name=f"pairs{t}", tag=f"pairs{t}", align_bytes=64))
            nc.scalar.activation(pairs[t][:, 0, :], h_rows[t][:].indirect(n1_sb[:]), ACT.Copy, scale=0.5)
            nc.scalar.activation(pairs[t][:, 1, :], h_rows[t][:].indirect(n2_sb[:]), ACT.Copy, scale=-0.5)
            lead = sb.tile([P, W], F32, name=f"lead{t}")
            nc.vector.tensor_tensor(lead[:], pairs[t][:, 0, :], pairs[t][:, 1, :], ALU.add)
            sig.append(lead)

        def weigh(t):
            share = sb.tile([P, W], F32, name=f"share{t}")
            nc.scalar.activation(share[:], sig[t][:], ACT.Tanh)
            duel.append(sb.tile([P, 2, W], F32, name=f"duel{t}"))
            nc.vector.scalar_tensor_tensor(duel[t][:, 0, :], share[:], 1.0, pairs[t][:, 0, :], ALU.add, ALU.mult)
            nc.vector.scalar_tensor_tensor(duel[t][:, 1, :], share[:], 1.0, pairs[t][:, 1, :], ALU.subtract, ALU.mult)

        def put_back(t):
            dt_rows.append(sb.tile([P, S], F32, name=f"dt_rows{t}"))
            nc.scalar.activation(dt_rows[t][:].indirect(n1_sb[:]), duel[t][:, 0, :], ACT.Copy)
            nc.scalar.activation(dt_rows[t][:].indirect(n2_sb[:]), duel[t][:, 1, :], ACT.Copy)

        def group(t, cols):
            nc.vector.tensor_scalar(z_grouped[:, cols, t], dt_rows[t][:, cols], gain[:, t : t + 1], None, ALU.mult)


        for step in range(PACK + 2):
            if step < PACK:
                fetch_pairs(step)
            if 1 <= step <= PACK:
                weigh(step - 1)
            if step >= 2:
                put_back(step - 2)
                if step - 2 < PACK - 1:
                    group(step - 2, slice(0, S))
            if step == 3:
                xc_bytes = sb.tile([P, C], U8, name="xc_bytes", tag="pairs2", align_bytes=64)
                nc.vector.tensor_copy(xc_bytes[:], x_bytes[:].indirect(cand_sb[:]))
                xc_plane = sb.tile([P, C], U8, name="xc_plane", align_bytes=64)
                to_plane(xc_plane, xc_bytes, (nc.sync,) * 4)
            if step == 4:
                xc_words = sb.tile([P, C], U32, name="xc_words", tag="pairs3", align_bytes=64)
                nc.vector.tensor_copy(xc_words[:], x_table[:].indirect(cand_sb[:]))

        z_words = sb.tile([P, S], U32, name="z_words", align_bytes=64)
        z_plane = sb.tile([P, S], U8, name="z_plane", align_bytes=64)
        for cols in halves:
            group(PACK - 1, cols)
        for cols in halves:
            nc.vector.quantize_mx(
                out=z_words[:, cols].bitcast(FP8X4), scales=z_plane[:, cols],
                in_=z_grouped[:, cols, :].rearrange("p w t -> p (w t)"),
            )

        def score(c, cols, tag):
            rows = slice(c * P, (c + 1) * P)
            acc = psum.tile([P, cols.stop - cols.start], F32, name=f"s_acc{c}_{cols.start}", tag=tag)
            nc.tensor.matmul_mx(
                out=acc[:], lhsT=xc_words[:, rows].bitcast(FP8X4), lhsT_scale=xc_plane[:, rows],
                rhs=z_words[:, cols].bitcast(FP8X4), rhs_scale=z_plane[:, cols], start=True, stop=True,
            )
            return acc

        nc.scalar.activation(s_rows[0][:, halves[0]], score(0, halves[0], "s_acc0")[:], ACT.Copy, scale=0.0625)
        nc.vector.tensor_scalar(s_rows[0][:, halves[1]], score(0, halves[1], "h_acc0")[:], 0.0625, None, ALU.mult)
        for c in range(1, C // P):
            nc.vector.tensor_scalar(s_rows[c][:, :S], score(c, slice(0, S), f"s_acc{c}")[:], 0.0625, None, ALU.mult)

        last = C // P - 1
        pending = []
        for c in range(C // P):
            mb = sb.tile([P, S, MEMBERS], F32, name=f"mb{c}")
            low2 = sb.tile([P, S, 2], F32, name=f"low2_{c}")
            high2 = sb.tile([P, S, 2], F32, name=f"high2_{c}")
            low = sb.tile([P, S], F32, name=f"low{c}")
            high = sb.tile([P, S], F32, name=f"high{c}")
            kept = sb.tile([P, S], F32, name=f"kept{c}")
            result = sb.tile([P, S], F32, name=f"result{c}")

            def finish(cols, c=c, high=high, kept=kept, result=result):
                nc.vector.scalar_tensor_tensor(result[:, cols], high[:, cols], -0.5, kept[:, cols], ALU.mult, ALU.add)
                queue = nc.scalar if c == last and cols.stop == S else nc.sync
                queue.dma_start(out[c * P : (c + 1) * P, cols], result[:, cols])

            cuts = (0, S // 4, S // 2, S) if c == 0 else (0, S // 2, S)
            done = 0
            for j0, j1 in zip(cuts, cuts[1:]):
                nc.scalar.activation(
                    mb[:, j0:j1, :].rearrange("p j t -> p (j t)"),
                    s_rows[c][:].indirect(n3_sb[:, j0 * MEMBERS // 16 : j1 * MEMBERS // 16]),
                    ACT.Copy,
                )
                nc.vector.tensor_tensor(low2[:, j0:j1, :], mb[:, j0:j1, 0::2], mb[:, j0:j1, 1::2], ALU.min)
                for call, cols in pending:
                    call(cols)
                pending.clear()
                nc.vector.tensor_tensor(high2[:, j0:j1, :], mb[:, j0:j1, 0::2], mb[:, j0:j1, 1::2], ALU.max)
                if j1 == S or (c == 0 and j1 == S // 2):
                    cols = slice(done, j1)
                    done = j1
                    nc.vector.tensor_tensor(low[:, cols], low2[:, cols, 0], low2[:, cols, 1], ALU.min)
                    nc.vector.tensor_tensor(high[:, cols], high2[:, cols, 0], high2[:, cols, 1], ALU.max)
                    for part in halves if c == last else [cols]:
                        nc.vector.tensor_tensor(kept[:, part], low[:, part], s_rows[c][:, part], ALU.max)
                        pending.append((finish, part))
        for call, cols in pending:
            call(cols)
